import numpy as np
import ml_dtypes


def mxq(x, axis, fmt="e4m3"):
    dtype, down = {"e4m3": (ml_dtypes.float8_e4m3fn, 7), "e5m2": (ml_dtypes.float8_e5m2, 14)}[fmt]
    v = np.moveaxis(np.asarray(x, np.float32).astype(ml_dtypes.bfloat16).astype(np.float64), axis, -1)
    blocks = v.reshape(v.shape[:-1] + (-1, 32))
    amax = np.abs(blocks).max(-1, keepdims=True)
    byte = np.maximum(np.where(amax > 0, np.frexp(amax)[1] - 1 + 127, 0) - down, 1)
    scale = np.exp2(byte - 127.0)
    codes = (blocks / scale).astype(np.float32).astype(dtype).astype(np.float64)
    return np.moveaxis((codes * scale).reshape(v.shape), -1, axis)


WIDE = False


def mx_kscale(k):
    if not WIDE:
        return np.ones(k)
    levels = np.array([10, -10, 5, -5, 0])
    if k % 512:
        return np.exp2(np.random.permutation(np.resize(levels, k // 32))).repeat(32)
    a = np.empty((k // 512, 16))
    for p in range(k // 512):
        a[p, :8] = np.random.permutation(np.resize(levels, 8))
        for g in range(8):
            far = levels[np.abs(levels - a[p, g]) >= 10]
            a[p, g + 8] = far[np.random.randint(len(far))]
    return np.exp2(a.ravel()).repeat(32)


BF16 = ml_dtypes.bfloat16


def bf(x):
    return np.asarray(x, np.float32).astype(BF16)


def f64(x):
    return np.asarray(x).astype(np.float64)


E, C = 1536, 512

THIRD = 0.35


def setup_inputs():
    s = mx_kscale(E)
    return {
        "flow": bf(np.random.standard_normal((E, C)) / s[:, None]),
        "low": bf(THIRD * np.random.standard_normal((E, E)) / np.sqrt(E) * s),
        "up": bf(THIRD * np.random.standard_normal((E, E)) / np.sqrt(E) * s),
        "a": bf((1 + 0.1 * np.random.standard_normal(E)) / s),
        "b": bf((1 + 0.1 * np.random.standard_normal(E)) / s),
        "g": bf((1 + 0.1 * np.random.standard_normal(E)) * s),
    }


def reference(flow, low, up, a, b, g):
    x = f64(flow)
    lq = mxq(f64(low), 1, "e4m3")
    uq = mxq(f64(up), 1, "e4m3")
    x1 = x + f64(a)[:, None] * (lq @ mxq(x, 0, "e4m3"))
    x2 = x1 + f64(b)[:, None] * (uq @ mxq(x1, 0, "e4m3"))
    return f64(g)[:, None] * x2 + (lq @ mxq(x2, 0, "e4m3"))

@@ -1,0 +1,211 @@
+from contextlib import ExitStack
+
+import concourse.mybir as mybir
+from concourse.masks import make_identity
+
+E, C = 1536, 512
+FLOPS = 3 * 2 * E * E * C
+
+F32 = mybir.dt.float32
+BF16 = mybir.dt.bfloat16
+U32 = mybir.dt.uint32
+U8 = mybir.dt.uint8
+FP8X4 = mybir.dt.float8_e4m3fn_x4
+MULT = mybir.AluOpType.mult
+ADD = mybir.AluOpType.add
+
+P = 128
+PACK = 4
+K_PASS = P * PACK
+PASSES = E // K_PASS
+TILES = E // P
+WORDS = K_PASS // 2
+HEAD_SPLIT = 384
+LAST_SPLIT = 320
+DEFERRED = 5
+
+
+def unit_order():
+    first = [(t, g) for g in range(PASSES) for t in range(PACK)]
+    rest = [(m, g) for m in range(PACK, TILES) for g in range(PASSES)]
+    return first + rest
+
+
+def tile_simplicial_edge_flow_filter_t1_kernel(tc, flow, low, up, a, b, g, out):
+    nc = tc.nc
+    with ExitStack() as ctx:
+        keep = ctx.enter_context(tc.tile_pool(name="keep", bufs=1))
+        stage = ctx.enter_context(tc.tile_pool(name="stage", bufs=3))
+        psum = ctx.enter_context(tc.psum_pool(name="psum", bufs=4))
+        ctx.enter_context(tc.manual_schedule())
+
+        ident = keep.tile([P, P], F32, name="ident")
+        make_identity(nc, ident[:])
+
+        raw = {}
+        flow_sb = []
+        step = {}
+
+        def load_block(name, mat, k):
+            blk = keep.tile([P, PACK, K_PASS], BF16, name="%s_blk%d" % (name, k), align_bytes=64)
+            src = mat[0:K_PASS, k * K_PASS : (k + 1) * K_PASS].rearrange("(p t) k -> p t k", t=PACK)
+            nc.sync.dma_start(out=blk[:], in_=src)
+            for t in range(PACK):
+                raw[name, t, k] = blk[:, t, :].bitcast(F32)
+
+        def load_rows(name, mat, m):
+            grp, t = divmod(m, PACK)
+            rows = keep.tile([P, E], BF16, name="%s_rows%d" % (name, m), align_bytes=64)
+            src = mat[grp * K_PASS : (grp + 1) * K_PASS, :].rearrange("(p t) k -> p t k", t=PACK)
+            nc.sync.dma_start(out=rows[:], in_=src[:, t, :])
+            for k in range(PASSES):
+                raw[name, m, k] = rows[:, k * K_PASS : (k + 1) * K_PASS].bitcast(F32)
+
+        def load_flow(k):
+            rows = keep.tile([P, PACK, C], BF16, name="flow%d" % k, align_bytes=64)
+            nc.sync.dma_start(
+                out=rows[:], in_=flow[k * K_PASS : (k + 1) * K_PASS, :].rearrange("(p t) c -> p t c", t=PACK)
+            )
+            flow_sb.append(rows)
+
+        def load_step(name, vec):
+            cols = keep.tile([P, PASSES, PACK], BF16, name="step_%s" % name)
+            nc.sync.dma_start(out=cols[:], in_=vec.rearrange("(k p t) -> p k t", p=P, t=PACK))
+            step[name] = cols
+
+        for k in range(PASSES):
+            load_block("low", low, k)
+            load_flow(k)
+        load_step("a", a)
+        for m in range(PACK, TILES):
+            load_rows("low", low, m)
+        load_step("b", b)
+        load_step("g", g)
+        for k in range(PASSES):
+            load_block("up", up, k)
+        for m in range(PACK, TILES):
+            load_rows("up", up, m)
+
+        state = [keep.tile([P, PACK, C], F32, name="state%d" % k) for k in range(PASSES)]
+        weight = {}
+        moving = {}
+        acc = {}
+
+        def turn_pair(name, units):
+            bank = psum.tile([P, 2, 2, P], F32, name="bank", tag="turn")
+            for i, (m, k) in enumerate(units):
+                for u in range(2):
+                    nc.tensor.transpose(bank[:, i, u, :], raw[name, m, k][:, u:WORDS:2], ident[:])
+            grouped = stage.tile([P, 2 * K_PASS], BF16, name="w_grouped", tag="w_grouped", bufs=4, align_bytes=64)
+            nc.scalar.copy(
+                out=grouped[:].bitcast(F32).rearrange("p (i r u) -> p i r u", i=2, u=2),
+                in_=bank[:].rearrange("p i u r -> p i r u"),
+            )
+            return grouped
+
+        def quantize_pair(name, units, grouped):
+            label = "%s_%d_%d" % (name, units[0][0], units[0][1])
+            codes = keep.tile([P, 2 * P], U32, name="wc_" + label, align_bytes=64)
+            scales = keep.tile([P, 2 * P], U8, name="ws_" + label, align_bytes=64)
+            nc.vector.quantize_mx(out=codes[:].bitcast(FP8X4), scales=scales[:], in_=grouped[:])
+            for i, (m, k) in enumerate(units):
+                weight[name, m, k] = (codes[:, i * P : (i + 1) * P], scales[:, i * P : (i + 1) * P])
+
+        def interleave(src, split):
+            grouped = stage.tile([P, C, PACK], BF16, name="x_grouped", tag="x_grouped", align_bytes=64)
+            dst = grouped[:].rearrange("p (c i) t -> p c t i", i=4)
+            runs = src[:].rearrange("p t (c i) -> p c t i", i=4)
+            if split < C:
+                nc.scalar.copy(out=dst[:, split // 4 :], in_=runs[:, split // 4 :])
+            nc.vector.tensor_copy(out=dst[:, : split // 4], in_=runs[:, : split // 4])
+            return grouped
+
+        def quantize_state(s, k, grouped):
+            codes = keep.tile([P, C], U32, name="xc_%d_%d" % (s, k), align_bytes=64)
+            scales = keep.tile([P, C], U8, name="xs_%d_%d" % (s, k), align_bytes=64)
+            nc.vector.quantize_mx(
+                out=codes[:].bitcast(FP8X4), scales=scales[:], in_=grouped[:].rearrange("p c t -> p (c t)")
+            )
+            moving[s, k] = (codes, scales)
+
+        def product(s, name, m, k, tag):
+            if k == 0:
+                acc[s, m] = psum.tile([P, C], F32, name="acc", tag=tag)
+            w_codes, w_scales = weight[name, m, k]
+            x_codes, x_scales = moving[s, k]
+            nc.tensor.matmul_mx(
+                out=acc[s, m][:],
+                lhsT=w_codes.bitcast(FP8X4),
+                lhsT_scale=w_scales,
+                rhs=x_codes[:].bitcast(FP8X4),
+                rhs_scale=x_scales[:],
+                start=(k == 0),
+                stop=(k == PASSES - 1),
+            )
+
+        def correct(s, m):
+            grp, t = divmod(m, PACK)
+            before = flow_sb[grp] if s == 0 else state[grp]
+            nc.vector.scalar_tensor_tensor(
+                out=state[grp][:, t, :],
+                in0=acc[s, m][:],
+                scalar=step["a" if s == 0 else "b"][:, grp, t : t + 1],
+                in1=before[:, t, :],
+                op0=MULT,
+                op1=ADD,
+            )
+
+        def finish(m):
+            grp, t = divmod(m, PACK)
+            nc.vector.scalar_tensor_tensor(
+                out=state[grp][:, t, :],
+                in0=state[grp][:, t, :],
+                scalar=step["g"][:, grp, t : t + 1],
+                in1=acc[2, m][:],
+                op0=MULT,
+                op1=ADD,
+            )
+            dst = out[grp * K_PASS : (grp + 1) * K_PASS, :].rearrange("(p t) c -> p t c", t=PACK)
+            nc.sync.dma_start(out=dst[:, t, :], in_=state[grp][:, t, :])
+
+        order = unit_order()
+        rounds = [
+            (s, name, order[i : i + 4]) for s, name in enumerate(("low", "up")) for i in range(0, len(order), 4)
+        ]
+        complete = None
+        for j in range(len(rounds) + 1):
+            flow_grouped = interleave(flow_sb[j], HEAD_SPLIT) if j < PASSES else None
+            if j < len(rounds):
+                s, name, units = rounds[j]
+                first = turn_pair(name, units[:2])
+                second = turn_pair(name, units[2:])
+                quantize_pair(name, units[:2], first)
+                if flow_grouped is not None:
+                    quantize_state(0, j, flow_grouped)
+                quantize_pair(name, units[2:], second)
+            pending = None
+            if complete is not None:
+                pending = (complete, interleave(state[complete[1]], C))
+                complete = None
+            if j > 0:
+                s, name, units = rounds[j - 1]
+                for m, k in units:
+                    product(s, name, m, k, "acc")
+                for m, k in units:
+                    if k == PASSES - 1:
+                        correct(s, m)
+                        if m % PACK == PACK - 1:
+                            complete = (s + 1, m // PACK)
+            if pending is not None:
+                quantize_state(pending[0][0], pending[0][1], pending[1])
+
+        last = interleave(state[PASSES - 1], LAST_SPLIT)
+        quantize_state(2, PASSES - 1, last)
+        tags = ["turn" if (m // PACK) % 2 == 0 else "acc" for m in range(TILES)]
+        for m in range(DEFERRED):
+            for k in range(PASSES - 1):
+                product(2, "low", m, k, tags[m])
+        for m in range(TILES):
+            for k in range(PASSES - 1 if m < DEFERRED else 0, PASSES):
+                product(2, "low", m, k, tags[m])
+            finish(m)

@@ -22,7 +22,18 @@ TILES = E // P
 WORDS = K_PASS // 2
 HEAD_SPLIT = 384
 LAST_SPLIT = 320
-DEFERRED = 5
+DEFERRED = 6
+ROUND = 6
+L_ROUNDS = [4, 4, 4, 6, 6, 6, 6]
+LATE_SPLIT = 0
+LATE_FROM = 12
+SORT_FROM = 5
+SORT_N = 4
+SORT_AHEAD = 2
+MID_SPLIT = 512
+WARM = [3, 5, 0, 0]
+HEAD = "c0 d0 x0 b1 x1 b2 x2"
+HALVES = 1
 
 
 def unit_order():
@@ -46,12 +57,12 @@ def tile_simplicial_edge_flow_filter_t1_kernel(tc, flow, low, up, a, b, g, out):
         flow_sb = []
         step = {}
 
-        def load_block(name, mat, k):
-            blk = keep.tile([P, PACK, K_PASS], BF16, name="%s_blk%d" % (name, k), align_bytes=64)
+        def load_block(name, mat, k, t0, t1):
+            blk = keep.tile([P, t1 - t0, K_PASS], BF16, name="%s_blk%d_%d" % (name, k, t0), align_bytes=64)
             src = mat[0:K_PASS, k * K_PASS : (k + 1) * K_PASS].rearrange("(p t) k -> p t k", t=PACK)
-            nc.sync.dma_start(out=blk[:], in_=src)
-            for t in range(PACK):
-                raw[name, t, k] = blk[:, t, :].bitcast(F32)
+            nc.sync.dma_start(out=blk[:], in_=src[:, t0:t1, :])
+            for t in range(t0, t1):
+                raw[name, t, k] = blk[:, t - t0, :].bitcast(F32)
 
         def load_rows(name, mat, m):
             grp, t = divmod(m, PACK)
@@ -73,16 +84,27 @@ def tile_simplicial_edge_flow_filter_t1_kernel(tc, flow, low, up, a, b, g, out):
             nc.sync.dma_start(out=cols[:], in_=vec.rearrange("(k p t) -> p k t", p=P, t=PACK))
             step[name] = cols
 
-        for k in range(PASSES):
-            load_block("low", low, k)
-            load_flow(k)
+        early = 0
+        for item in HEAD.split():
+            k = int(item[1])
+            if item[0] == "b":
+                load_block("low", low, k, 0, PACK)
+            elif item[0] == "c":
+                load_block("low", low, k, 0, 2)
+            elif item[0] == "d":
+                load_block("low", low, k, 2, PACK)
+            elif item[0] == "r":
+                load_rows("low", low, k)
+                early = early + 1
+            else:
+                load_flow(k)
         load_step("a", a)
-        for m in range(PACK, TILES):
+        for m in range(PACK + early, TILES):
             load_rows("low", low, m)
         load_step("b", b)
         load_step("g", g)
         for k in range(PASSES):
-            load_block("up", up, k)
+            load_block("up", up, k, 0, PACK)
         for m in range(PACK, TILES):
             load_rows("up", up, m)
 
@@ -91,12 +113,45 @@ def tile_simplicial_edge_flow_filter_t1_kernel(tc, flow, low, up, a, b, g, out):
         moving = {}
         acc = {}
 
+        halved = {}
+
+        def sort_words(name, m, k):
+            words = stage.tile([P, WORDS], F32, name="halved", tag="halved", bufs=SORT_N * (SORT_AHEAD + 1))
+            nc.scalar.copy(
+                out=words[:].rearrange("p (u q i) -> p q u i", u=2, i=4),
+                in_=raw[name, m, k].rearrange("p (q i u) -> p q u i", u=2, i=4),
+            )
+            halved[name, m, k] = words
+
+        warm_in = keep.tile([P, PACK * C], BF16, name="warm_in", align_bytes=64)
+        warm_codes = keep.tile([P, C], U32, name="warm_codes", align_bytes=64)
+        warm_scales = keep.tile([P, C], U8, name="warm_scales", align_bytes=64)
+        nc.vector.memset(warm_in[:].bitcast(U32), 0)
+        nc.vector.quantize_mx(out=warm_codes[:].bitcast(FP8X4), scales=warm_scales[:], in_=warm_in[:])
+
+        def warm(count):
+            for i in range(count):
+                junk = psum.tile([P, C], F32, name="junk", tag="acc")
+                nc.tensor.matmul_mx(
+                    out=junk[:],
+                    lhsT=warm_codes[:, :P].bitcast(FP8X4),
+                    lhsT_scale=warm_scales[:, :P],
+                    rhs=warm_codes[:].bitcast(FP8X4),
+                    rhs_scale=warm_scales[:],
+                    start=True,
+                    stop=True,
+                )
+
         def turn_pair(name, units):
             bank = psum.tile([P, 2, 2, P], F32, name="bank", tag="turn")
             for i, (m, k) in enumerate(units):
                 for u in range(2):
-                    nc.tensor.transpose(bank[:, i, u, :], raw[name, m, k][:, u:WORDS:2], ident[:])
-            grouped = stage.tile([P, 2 * K_PASS], BF16, name="w_grouped", tag="w_grouped", bufs=4, align_bytes=64)
+                    if (name, m, k) in halved:
+                        words = halved[name, m, k][:, u * P : (u + 1) * P]
+                    else:
+                        words = raw[name, m, k][:, u:WORDS:2]
+                    nc.tensor.transpose(bank[:, i, u, :], words, ident[:])
+            grouped = stage.tile([P, 2 * K_PASS], BF16, name="w_grouped", tag="w_grouped", bufs=6, align_bytes=64)
             nc.scalar.copy(
                 out=grouped[:].bitcast(F32).rearrange("p (i r u) -> p i r u", i=2, u=2),
                 in_=bank[:].rearrange("p i u r -> p i r u"),
@@ -117,7 +172,8 @@ def tile_simplicial_edge_flow_filter_t1_kernel(tc, flow, low, up, a, b, g, out):
             runs = src[:].rearrange("p t (c i) -> p c t i", i=4)
             if split < C:
                 nc.scalar.copy(out=dst[:, split // 4 :], in_=runs[:, split // 4 :])
-            nc.vector.tensor_copy(out=dst[:, : split // 4], in_=runs[:, : split // 4])
+            if split > 0:
+                nc.vector.tensor_copy(out=dst[:, : split // 4], in_=runs[:, : split // 4])
             return grouped
 
         def quantize_state(s, k, grouped):
@@ -128,17 +184,17 @@ def tile_simplicial_edge_flow_filter_t1_kernel(tc, flow, low, up, a, b, g, out):
             )
             moving[s, k] = (codes, scales)
 
-        def product(s, name, m, k, tag):
+        def product(s, name, m, k, tag, c0=0, c1=C):
             if k == 0:
-                acc[s, m] = psum.tile([P, C], F32, name="acc", tag=tag)
+                acc[s, m] = psum.tile([P, c1 - c0], F32, name="acc", tag=tag)
             w_codes, w_scales = weight[name, m, k]
             x_codes, x_scales = moving[s, k]
             nc.tensor.matmul_mx(
                 out=acc[s, m][:],
                 lhsT=w_codes.bitcast(FP8X4),
                 lhsT_scale=w_scales,
-                rhs=x_codes[:].bitcast(FP8X4),
-                rhs_scale=x_scales[:],
+                rhs=x_codes[:, c0:c1].bitcast(FP8X4),
+                rhs_scale=x_scales[:, c0:c1],
                 start=(k == 0),
                 stop=(k == PASSES - 1),
             )
@@ -155,57 +211,74 @@ def tile_simplicial_edge_flow_filter_t1_kernel(tc, flow, low, up, a, b, g, out):
                 op1=ADD,
             )
 
-        def finish(m):
+        def finish(m, c0, c1):
             grp, t = divmod(m, PACK)
             nc.vector.scalar_tensor_tensor(
-                out=state[grp][:, t, :],
-                in0=state[grp][:, t, :],
+                out=state[grp][:, t, c0:c1],
+                in0=state[grp][:, t, c0:c1],
                 scalar=step["g"][:, grp, t : t + 1],
                 in1=acc[2, m][:],
                 op0=MULT,
                 op1=ADD,
             )
             dst = out[grp * K_PASS : (grp + 1) * K_PASS, :].rearrange("(p t) c -> p t c", t=PACK)
-            nc.sync.dma_start(out=dst[:, t, :], in_=state[grp][:, t, :])
+            nc.sync.dma_start(out=dst[:, t, c0:c1], in_=state[grp][:, t, c0:c1])
 
         order = unit_order()
-        rounds = [
-            (s, name, order[i : i + 4]) for s, name in enumerate(("low", "up")) for i in range(0, len(order), 4)
-        ]
-        complete = None
+        rounds = [(0, "low", order[sum(L_ROUNDS[:i]) : sum(L_ROUNDS[: i + 1])]) for i in range(len(L_ROUNDS))]
+        rounds = rounds + [(1, "up", order[i : i + ROUND]) for i in range(0, len(order), ROUND)]
+        complete = []
+        made = 0
         for j in range(len(rounds) + 1):
-            flow_grouped = interleave(flow_sb[j], HEAD_SPLIT) if j < PASSES else None
+            if j < len(WARM):
+                warm(WARM[j])
+            turned = []
             if j < len(rounds):
                 s, name, units = rounds[j]
-                first = turn_pair(name, units[:2])
-                second = turn_pair(name, units[2:])
-                quantize_pair(name, units[:2], first)
-                if flow_grouped is not None:
-                    quantize_state(0, j, flow_grouped)
-                quantize_pair(name, units[2:], second)
-            pending = None
-            if complete is not None:
-                pending = (complete, interleave(state[complete[1]], C))
-                complete = None
+                pairs = [units[i : i + 2] for i in range(0, len(units), 2)]
+                for pair in pairs:
+                    fresh = []
+                    while made < PASSES and s == 0 and made <= max(k for m, k in pair):
+                        fresh.append((made, interleave(flow_sb[made], HEAD_SPLIT)))
+                        made = made + 1
+                    grouped = turn_pair(name, pair)
+                    quantize_pair(name, pair, grouped)
+                    for k, gr in fresh:
+                        quantize_state(0, k, gr)
+            if SORT_FROM <= j + SORT_AHEAD < len(rounds):
+                s, name, units = rounds[j + SORT_AHEAD]
+                for m, k in units[:SORT_N]:
+                    sort_words(name, m, k)
+            pending = [(s, k, interleave(state[k], MID_SPLIT if j < LATE_FROM else LATE_SPLIT)) for s, k in complete]
+            complete = []
             if j > 0:
                 s, name, units = rounds[j - 1]
                 for m, k in units:
                     product(s, name, m, k, "acc")
-                for m, k in units:
                     if k == PASSES - 1:
                         correct(s, m)
                         if m % PACK == PACK - 1:
-                            complete = (s + 1, m // PACK)
-            if pending is not None:
-                quantize_state(pending[0][0], pending[0][1], pending[1])
+                            complete.append((s + 1, m // PACK))
+            if j == len(rounds) - 1:
+                held = pending
+                pending = []
+            for s, k, gr in pending:
+                quantize_state(s, k, gr)
 
+        for s, k, gr in held:
+            quantize_state(s, k, gr)
         last = interleave(state[PASSES - 1], LAST_SPLIT)
         quantize_state(2, PASSES - 1, last)
         tags = ["turn" if (m // PACK) % 2 == 0 else "acc" for m in range(TILES)]
-        for m in range(DEFERRED):
-            for k in range(PASSES - 1):
+        for k in range(PASSES - 1):
+            for m in range(DEFERRED):
                 product(2, "low", m, k, tags[m])
-        for m in range(TILES):
+        for m in range(TILES - HALVES):
             for k in range(PASSES - 1 if m < DEFERRED else 0, PASSES):
                 product(2, "low", m, k, tags[m])
-            finish(m)
+            finish(m, 0, C)
+        for m in range(TILES - HALVES, TILES):
+            for c0 in range(0, C, C // 2):
+                for k in range(PASSES):
+                    product(2, "low", m, k, "turn", c0, c0 + C // 2)
+                finish(m, c0, c0 + C // 2)

from contextlib import ExitStack

import concourse.mybir as mybir
from concourse.masks import make_identity

E, C = 1536, 512
FLOPS = 3 * 2 * E * E * C

F32 = mybir.dt.float32
BF16 = mybir.dt.bfloat16
U32 = mybir.dt.uint32
U8 = mybir.dt.uint8
FP8X4 = mybir.dt.float8_e4m3fn_x4
MULT = mybir.AluOpType.mult
ADD = mybir.AluOpType.add

P = 128
PACK = 4
K_PASS = P * PACK
PASSES = E // K_PASS
TILES = E // P
WORDS = K_PASS // 2
HEAD_SPLIT = 384
LAST_SPLIT = 320
DEFERRED = 6
ROUND = 6
L_ROUNDS = [4, 4, 4, 6, 6, 6, 6]
LATE_SPLIT = 0
LATE_FROM = 12
SORT_FROM = 5
SORT_N = 4
SORT_AHEAD = 2
MID_SPLIT = 512
WARM = [3, 5, 0, 0]
HEAD = "c0 d0 x0 b1 x1 b2 x2"
HALVES = 1


def unit_order():
    first = [(t, g) for g in range(PASSES) for t in range(PACK)]
    rest = [(m, g) for m in range(PACK, TILES) for g in range(PASSES)]
    return first + rest


def tile_simplicial_edge_flow_filter_t1_kernel(tc, flow, low, up, a, b, g, out):
    nc = tc.nc
    with ExitStack() as ctx:
        keep = ctx.enter_context(tc.tile_pool(name="keep", bufs=1))
        stage = ctx.enter_context(tc.tile_pool(name="stage", bufs=3))
        psum = ctx.enter_context(tc.psum_pool(name="psum", bufs=4))
        ctx.enter_context(tc.manual_schedule())

        ident = keep.tile([P, P], F32, name="ident")
        make_identity(nc, ident[:])

        raw = {}
        flow_sb = []
        step = {}

        def load_block(name, mat, k, t0, t1):
            blk = keep.tile([P, t1 - t0, K_PASS], BF16, name="%s_blk%d_%d" % (name, k, t0), align_bytes=64)
            src = mat[0:K_PASS, k * K_PASS : (k + 1) * K_PASS].rearrange("(p t) k -> p t k", t=PACK)
            nc.sync.dma_start(out=blk[:], in_=src[:, t0:t1, :])
            for t in range(t0, t1):
                raw[name, t, k] = blk[:, t - t0, :].bitcast(F32)

        def load_rows(name, mat, m):
            grp, t = divmod(m, PACK)
            rows = keep.tile([P, E], BF16, name="%s_rows%d" % (name, m), align_bytes=64)
            src = mat[grp * K_PASS : (grp + 1) * K_PASS, :].rearrange("(p t) k -> p t k", t=PACK)
            nc.sync.dma_start(out=rows[:], in_=src[:, t, :])
            for k in range(PASSES):
                raw[name, m, k] = rows[:, k * K_PASS : (k + 1) * K_PASS].bitcast(F32)

        def load_flow(k):
            rows = keep.tile([P, PACK, C], BF16, name="flow%d" % k, align_bytes=64)
            nc.sync.dma_start(
                out=rows[:], in_=flow[k * K_PASS : (k + 1) * K_PASS, :].rearrange("(p t) c -> p t c", t=PACK)
            )
            flow_sb.append(rows)

        def load_step(name, vec):
            cols = keep.tile([P, PASSES, PACK], BF16, name="step_%s" % name)
            nc.sync.dma_start(out=cols[:], in_=vec.rearrange("(k p t) -> p k t", p=P, t=PACK))
            step[name] = cols

        early = 0
        for item in HEAD.split():
            k = int(item[1])
            if item[0] == "b":
                load_block("low", low, k, 0, PACK)
            elif item[0] == "c":
                load_block("low", low, k, 0, 2)
            elif item[0] == "d":
                load_block("low", low, k, 2, PACK)
            elif item[0] == "r":
                load_rows("low", low, k)
                early = early + 1
            else:
                load_flow(k)
        load_step("a", a)
        for m in range(PACK + early, TILES):
            load_rows("low", low, m)
        load_step("b", b)
        load_step("g", g)
        for k in range(PASSES):
            load_block("up", up, k, 0, PACK)
        for m in range(PACK, TILES):
            load_rows("up", up, m)

        state = [keep.tile([P, PACK, C], F32, name="state%d" % k) for k in range(PASSES)]
        weight = {}
        moving = {}
        acc = {}

        halved = {}

        def sort_words(name, m, k):
            words = stage.tile([P, WORDS], F32, name="halved", tag="halved", bufs=SORT_N * (SORT_AHEAD + 1))
            nc.scalar.copy(
                out=words[:].rearrange("p (u q i) -> p q u i", u=2, i=4),
                in_=raw[name, m, k].rearrange("p (q i u) -> p q u i", u=2, i=4),
            )
            halved[name, m, k] = words

        warm_in = keep.tile([P, PACK * C], BF16, name="warm_in", align_bytes=64)
        warm_codes = keep.tile([P, C], U32, name="warm_codes", align_bytes=64)
        warm_scales = keep.tile([P, C], U8, name="warm_scales", align_bytes=64)
        nc.vector.memset(warm_in[:].bitcast(U32), 0)
        nc.vector.quantize_mx(out=warm_codes[:].bitcast(FP8X4), scales=warm_scales[:], in_=warm_in[:])

        def warm(count):
            for i in range(count):
                junk = psum.tile([P, C], F32, name="junk", tag="acc")
                nc.tensor.matmul_mx(
                    out=junk[:],
                    lhsT=warm_codes[:, :P].bitcast(FP8X4),
                    lhsT_scale=warm_scales[:, :P],
                    rhs=warm_codes[:].bitcast(FP8X4),
                    rhs_scale=warm_scales[:],
                    start=True,
                    stop=True,
                )

        def turn_pair(name, units):
            bank = psum.tile([P, 2, 2, P], F32, name="bank", tag="turn")
            for i, (m, k) in enumerate(units):
                for u in range(2):
                    if (name, m, k) in halved:
                        words = halved[name, m, k][:, u * P : (u + 1) * P]
                    else:
                        words = raw[name, m, k][:, u:WORDS:2]
                    nc.tensor.transpose(bank[:, i, u, :], words, ident[:])
            grouped = stage.tile([P, 2 * K_PASS], BF16, name="w_grouped", tag="w_grouped", bufs=6, align_bytes=64)
            nc.scalar.copy(
                out=grouped[:].bitcast(F32).rearrange("p (i r u) -> p i r u", i=2, u=2),
                in_=bank[:].rearrange("p i u r -> p i r u"),
            )
            return grouped

        def quantize_pair(name, units, grouped):
            label = "%s_%d_%d" % (name, units[0][0], units[0][1])
            codes = keep.tile([P, 2 * P], U32, name="wc_" + label, align_bytes=64)
            scales = keep.tile([P, 2 * P], U8, name="ws_" + label, align_bytes=64)
            nc.vector.quantize_mx(out=codes[:].bitcast(FP8X4), scales=scales[:], in_=grouped[:])
            for i, (m, k) in enumerate(units):
                weight[name, m, k] = (codes[:, i * P : (i + 1) * P], scales[:, i * P : (i + 1) * P])

        def interleave(src, split):
            grouped = stage.tile([P, C, PACK], BF16, name="x_grouped", tag="x_grouped", align_bytes=64)
            dst = grouped[:].rearrange("p (c i) t -> p c t i", i=4)
            runs = src[:].rearrange("p t (c i) -> p c t i", i=4)
            if split < C:
                nc.scalar.copy(out=dst[:, split // 4 :], in_=runs[:, split // 4 :])
            if split > 0:
                nc.vector.tensor_copy(out=dst[:, : split // 4], in_=runs[:, : split // 4])
            return grouped

        def quantize_state(s, k, grouped):
            codes = keep.tile([P, C], U32, name="xc_%d_%d" % (s, k), align_bytes=64)
            scales = keep.tile([P, C], U8, name="xs_%d_%d" % (s, k), align_bytes=64)
            nc.vector.quantize_mx(
                out=codes[:].bitcast(FP8X4), scales=scales[:], in_=grouped[:].rearrange("p c t -> p (c t)")
            )
            moving[s, k] = (codes, scales)

        def product(s, name, m, k, tag, c0=0, c1=C):
            if k == 0:
                acc[s, m] = psum.tile([P, c1 - c0], F32, name="acc", tag=tag)
            w_codes, w_scales = weight[name, m, k]
            x_codes, x_scales = moving[s, k]
            nc.tensor.matmul_mx(
                out=acc[s, m][:],
                lhsT=w_codes.bitcast(FP8X4),
                lhsT_scale=w_scales,
                rhs=x_codes[:, c0:c1].bitcast(FP8X4),
                rhs_scale=x_scales[:, c0:c1],
                start=(k == 0),
                stop=(k == PASSES - 1),
            )

        def correct(s, m):
            grp, t = divmod(m, PACK)
            before = flow_sb[grp] if s == 0 else state[grp]
            nc.vector.scalar_tensor_tensor(
                out=state[grp][:, t, :],
                in0=acc[s, m][:],
                scalar=step["a" if s == 0 else "b"][:, grp, t : t + 1],
                in1=before[:, t, :],
                op0=MULT,
                op1=ADD,
            )

        def finish(m, c0, c1):
            grp, t = divmod(m, PACK)
            nc.vector.scalar_tensor_tensor(
                out=state[grp][:, t, c0:c1],
                in0=state[grp][:, t, c0:c1],
                scalar=step["g"][:, grp, t : t + 1],
                in1=acc[2, m][:],
                op0=MULT,
                op1=ADD,
            )
            dst = out[grp * K_PASS : (grp + 1) * K_PASS, :].rearrange("(p t) c -> p t c", t=PACK)
            nc.sync.dma_start(out=dst[:, t, c0:c1], in_=state[grp][:, t, c0:c1])

        order = unit_order()
        rounds = [(0, "low", order[sum(L_ROUNDS[:i]) : sum(L_ROUNDS[: i + 1])]) for i in range(len(L_ROUNDS))]
        rounds = rounds + [(1, "up", order[i : i + ROUND]) for i in range(0, len(order), ROUND)]
        complete = []
        made = 0
        for j in range(len(rounds) + 1):
            if j < len(WARM):
                warm(WARM[j])
            turned = []
            if j < len(rounds):
                s, name, units = rounds[j]
                pairs = [units[i : i + 2] for i in range(0, len(units), 2)]
                for pair in pairs:
                    fresh = []
                    while made < PASSES and s == 0 and made <= max(k for m, k in pair):
                        fresh.append((made, interleave(flow_sb[made], HEAD_SPLIT)))
                        made = made + 1
                    grouped = turn_pair(name, pair)
                    quantize_pair(name, pair, grouped)
                    for k, gr in fresh:
                        quantize_state(0, k, gr)
            if SORT_FROM <= j + SORT_AHEAD < len(rounds):
                s, name, units = rounds[j + SORT_AHEAD]
                for m, k in units[:SORT_N]:
                    sort_words(name, m, k)
            pending = [(s, k, interleave(state[k], MID_SPLIT if j < LATE_FROM else LATE_SPLIT)) for s, k in complete]
            complete = []
            if j > 0:
                s, name, units = rounds[j - 1]
                for m, k in units:
                    product(s, name, m, k, "acc")
                    if k == PASSES - 1:
                        correct(s, m)
                        if m % PACK == PACK - 1:
                            complete.append((s + 1, m // PACK))
            if j == len(rounds) - 1:
                held = pending
                pending = []
            for s, k, gr in pending:
                quantize_state(s, k, gr)

        for s, k, gr in held:
            quantize_state(s, k, gr)
        last = interleave(state[PASSES - 1], LAST_SPLIT)
        quantize_state(2, PASSES - 1, last)
        tags = ["turn" if (m // PACK) % 2 == 0 else "acc" for m in range(TILES)]
        for k in range(PASSES - 1):
            for m in range(DEFERRED):
                product(2, "low", m, k, tags[m])
        for m in range(TILES - HALVES):
            for k in range(PASSES - 1 if m < DEFERRED else 0, PASSES):
                product(2, "low", m, k, tags[m])
            finish(m, 0, C)
        for m in range(TILES - HALVES, TILES):
            for c0 in range(0, C, C // 2):
                for k in range(PASSES):
                    product(2, "low", m, k, "turn", c0, c0 + C // 2)
                finish(m, c0, c0 + C // 2)
